import numpy as np
import ml_dtypes


def mxq(x, axis, fmt="e4m3"):
    dtype, down = {"e4m3": (ml_dtypes.float8_e4m3fn, 7), "e5m2": (ml_dtypes.float8_e5m2, 14)}[fmt]
    v = np.moveaxis(np.asarray(x, np.float32).astype(ml_dtypes.bfloat16).astype(np.float64), axis, -1)
    blocks = v.reshape(v.shape[:-1] + (-1, 32))
    amax = np.abs(blocks).max(-1, keepdims=True)
    byte = np.maximum(np.where(amax > 0, np.frexp(amax)[1] - 1 + 127, 0) - down, 1)
    scale = np.exp2(byte - 127.0)
    codes = (blocks / scale).astype(np.float32).astype(dtype).astype(np.float64)
    return np.moveaxis((codes * scale).reshape(v.shape), -1, axis)


WIDE = False


def mx_kscale(k):
    if not WIDE:
        return np.ones(k)
    levels = np.array([10, -10, 5, -5, 0])
    if k % 512:
        return np.exp2(np.random.permutation(np.resize(levels, k // 32))).repeat(32)
    a = np.empty((k // 512, 16))
    for p in range(k // 512):
        a[p, :8] = np.random.permutation(np.resize(levels, 8))
        for g in range(8):
            far = levels[np.abs(levels - a[p, g]) >= 10]
            a[p, g + 8] = far[np.random.randint(len(far))]
    return np.exp2(a.ravel()).repeat(32)


def f64(x):
    return np.asarray(x).astype(np.float64)


def striped(idx):
    return np.tile(idx.reshape(-1, 16).T, (8, 1)).astype(np.uint16)


def unstriped(offs):
    return offs[:16].T.reshape(-1).astype(np.int64)


K, T, S, N = 1536, 2048, 768, 256


def setup_inputs():
    n = np.random.standard_normal
    s = mx_kscale(K)[:, None]
    return {
        "xT": (n((K, T)) * s).astype(np.float32),
        "w": (n((K, N)) / np.sqrt(K) / s).astype(np.float32),
        "offs": striped(np.sort(np.random.permutation(T)[:S])),
    }


def reference(xT, w, offs):
    idx = unstriped(offs)
    xq = mxq(f64(xT)[:, idx], 0, "e4m3")
    y = mxq(f64(w), 0, "e4m3").T @ xq
    return y

@@ -1,0 +1,127 @@
+from contextlib import ExitStack
+
+import concourse.mybir as mybir
+
+K, T, S, N = 1536, 2048, 768, 256
+FLOPS = 2 * K * S * N
+
+F32 = mybir.dt.float32
+BF16 = mybir.dt.bfloat16
+I32 = mybir.dt.int32
+U32 = mybir.dt.uint32
+U16 = mybir.dt.uint16
+U8 = mybir.dt.uint8
+FP8X4 = mybir.dt.float8_e4m3fn_x4
+COPY = mybir.ActivationFunctionType.Copy
+
+P = 128
+PACK = 4
+K_PASS = P * PACK
+PASSES = K // K_PASS
+M_TILE = 128
+SLICE = 256
+SLICES = S // SLICE
+
+
+def tile_picked_pick_lin_none_srt_e_kernel(tc, xT, w, offs, out):
+    nc = tc.nc
+    with ExitStack() as ctx:
+        keep = ctx.enter_context(tc.tile_pool(name="keep", bufs=1))
+        psum = ctx.enter_context(tc.psum_pool(name="psum", bufs=1))
+
+        offsets = keep.tile([P, S // 16], U16, name="offsets", align_bytes=64)
+        x_raw = [[keep.tile([P, T], F32, name=f"x_raw{a}{j}", align_bytes=64) for j in range(PACK)] for a in range(PASSES)]
+        g4 = [keep.tile([P, PACK, S], F32, name=f"g4_{a}", align_bytes=64) for a in range(PASSES)]
+        gb = [keep.tile([P, S, PACK], BF16, name=f"gb{a}", align_bytes=64) for a in range(PASSES)]
+        g_words = [keep.tile([P, S], U32, name=f"g_words{a}", align_bytes=64) for a in range(PASSES)]
+        g_bytes = [keep.tile([P, S], U8, name=f"g_bytes{a}", align_bytes=64) for a in range(PASSES)]
+        w_raw = keep.tile([P, PASSES, PACK, N], F32, name="w_raw", align_bytes=64)
+        w_bf = [keep.tile([P, N, PACK], BF16, name=f"w_bf{a}", align_bytes=64) for a in range(PASSES)]
+        w_words = [keep.tile([P, N], U32, name=f"w_words{a}", align_bytes=64) for a in range(PASSES)]
+        w_bytes = [keep.tile([P, N], U8, name=f"w_bytes{a}", align_bytes=64) for a in range(PASSES)]
+
+        def load_x(a, j, lo, hi):
+            rows = xT[a * K_PASS : (a + 1) * K_PASS, lo:hi].rearrange("(p j) c -> p j c", j=PACK)
+            nc.sync.dma_start(out=x_raw[a][j][:, lo:hi], in_=rows[:, j, :])
+
+        nc.sync.dma_start(offsets[:], offs)
+        for a in range(PASSES):
+            for j in range(PACK):
+                if (a, j) == (0, 2):
+                    nc.sync.dma_start(out=w_raw[:], in_=w.rearrange("(a p j) m -> p a j m", a=PASSES, j=PACK))
+                cuts = (0, T - 2 * SLICE, T - SLICE, T) if (a, j) == (PASSES - 1, PACK - 1) else (0, T)
+                for lo, hi in zip(cuts[:-1], cuts[1:]):
+                    load_x(a, j, lo, hi)
+
+        def cast(engine, dst, src, lo, hi):
+            o = dst[:, lo:hi, :].rearrange("p (c i) t -> p c t i", i=4)
+            i = src[:, :, lo:hi].rearrange("p t (c i) -> p c t i", i=4)
+            if engine == "s":
+                nc.scalar.activation(o, i, COPY)
+            else:
+                nc.vector.tensor_copy(o, i)
+
+        def quant(words, scales, bf, lo, hi):
+            nc.vector.quantize_mx(
+                out=words[:, lo:hi].bitcast(FP8X4),
+                scales=scales[:, lo:hi],
+                in_=bf[:, lo:hi, :].rearrange("p c t -> p (c t)"),
+            )
+
+        def gather(a, j, lo, hi, window):
+            picks = offsets[:, lo // 16 : hi // 16]
+            nc.vector.tensor_copy(g4[a][:, j, lo:hi], x_raw[a][j][:, 0:window].indirect(picks))
+
+        acc = {}
+        for s in range(SLICES):
+            for m in range(N // M_TILE):
+                acc[m, s] = psum.tile([M_TILE, SLICE], F32, name=f"acc{m}{s}")
+
+        def multiply(a, s):
+            for m in range(N // M_TILE):
+                mc = slice(m * M_TILE, (m + 1) * M_TILE)
+                jc = slice(s * SLICE, (s + 1) * SLICE)
+                nc.tensor.matmul_mx(
+                    out=acc[m, s][:],
+                    lhsT=w_words[a][:, mc].bitcast(FP8X4),
+                    lhsT_scale=w_bytes[a][:, mc],
+                    rhs=g_words[a][:, jc].bitcast(FP8X4),
+                    rhs_scale=g_bytes[a][:, jc],
+                    start=(a == 0),
+                    stop=(a == PASSES - 1),
+                )
+
+        def finish(s):
+            for m in range(N // M_TILE):
+                y = keep.tile([M_TILE, SLICE], F32, name=f"y{m}{s}")
+                if m == 0:
+                    nc.scalar.copy(y[:], acc[m, s][:])
+                else:
+                    nc.vector.tensor_copy(y[:], acc[m, s][:])
+                nc.sync.dma_start(out=out[m * M_TILE : (m + 1) * M_TILE, s * SLICE : (s + 1) * SLICE], in_=y[:])
+
+        for a in range(PASSES - 1):
+            for j in range(PACK):
+                gather(a, j, 0, S, T)
+            if a == 0:
+                for b in range(PASSES):
+                    cast("s", w_bf[b], w_raw[:, b, :, :], 0, N)
+                for b in range(PASSES):
+                    quant(w_words[b], w_bytes[b], w_bf[b], 0, N)
+            for lo, hi in ((0, 512), (512, 768)):
+                cast("s", gb[a], g4[a], lo, hi)
+                quant(g_words[a], g_bytes[a], gb[a], lo, hi)
+            for s in range(SLICES):
+                multiply(a, s)
+        a = PASSES - 1
+        for j in range(PACK - 1):
+            gather(a, j, 0, S, T)
+        for s in range(SLICES):
+            lo, hi = s * SLICE, (s + 1) * SLICE
+            gather(a, PACK - 1, lo, hi, T - S + hi)
+            cut = hi - SLICE // 2
+            cast("s", gb[a], g4[a], lo, cut)
+            cast("v", gb[a], g4[a], cut, hi)
+            quant(g_words[a], g_bytes[a], gb[a], lo, hi)
+            multiply(a, s)
+            finish(s)

@@ -35,27 +35,30 @@ def tile_picked_pick_lin_none_srt_e_kernel(tc, xT, w, offs, out):
         gb = [keep.tile([P, S, PACK], BF16, name=f"gb{a}", align_bytes=64) for a in range(PASSES)]
         g_words = [keep.tile([P, S], U32, name=f"g_words{a}", align_bytes=64) for a in range(PASSES)]
         g_bytes = [keep.tile([P, S], U8, name=f"g_bytes{a}", align_bytes=64) for a in range(PASSES)]
-        w_raw = keep.tile([P, PASSES, PACK, N], F32, name="w_raw", align_bytes=64)
+        w_raw = [keep.tile([P, PACK, N], F32, name=f"w_raw{a}", align_bytes=64) for a in range(PASSES)]
         w_bf = [keep.tile([P, N, PACK], BF16, name=f"w_bf{a}", align_bytes=64) for a in range(PASSES)]
         w_words = [keep.tile([P, N], U32, name=f"w_words{a}", align_bytes=64) for a in range(PASSES)]
         w_bytes = [keep.tile([P, N], U8, name=f"w_bytes{a}", align_bytes=64) for a in range(PASSES)]
+
+        def load_w(a):
+            nc.sync.dma_start(out=w_raw[a][:], in_=w[a * K_PASS : (a + 1) * K_PASS, :].rearrange("(p j) m -> p j m", j=PACK))
 
         def load_x(a, j, lo, hi):
             rows = xT[a * K_PASS : (a + 1) * K_PASS, lo:hi].rearrange("(p j) c -> p j c", j=PACK)
             nc.sync.dma_start(out=x_raw[a][j][:, lo:hi], in_=rows[:, j, :])
 
+        for a in range(PASSES):
+            load_w(a)
         nc.sync.dma_start(offsets[:], offs)
         for a in range(PASSES):
             for j in range(PACK):
-                if (a, j) == (0, 2):
-                    nc.sync.dma_start(out=w_raw[:], in_=w.rearrange("(a p j) m -> p a j m", a=PASSES, j=PACK))
                 cuts = (0, T - 2 * SLICE, T - SLICE, T) if (a, j) == (PASSES - 1, PACK - 1) else (0, T)
                 for lo, hi in zip(cuts[:-1], cuts[1:]):
                     load_x(a, j, lo, hi)
 
-        def cast(engine, dst, src, lo, hi):
-            o = dst[:, lo:hi, :].rearrange("p (c i) t -> p c t i", i=4)
-            i = src[:, :, lo:hi].rearrange("p t (c i) -> p c t i", i=4)
+        def cast(engine, dst, src, lo, hi, j0=0, j1=PACK):
+            o = dst[:, lo:hi, j0:j1].rearrange("p (c i) t -> p c t i", i=4)
+            i = src[:, j0:j1, lo:hi].rearrange("p t (c i) -> p c t i", i=4)
             if engine == "s":
                 nc.scalar.activation(o, i, COPY)
             else:
@@ -91,37 +94,48 @@ def tile_picked_pick_lin_none_srt_e_kernel(tc, xT, w, offs, out):
                     stop=(a == PASSES - 1),
                 )
 
-        def finish(s):
-            for m in range(N // M_TILE):
-                y = keep.tile([M_TILE, SLICE], F32, name=f"y{m}{s}")
-                if m == 0:
-                    nc.scalar.copy(y[:], acc[m, s][:])
-                else:
-                    nc.vector.tensor_copy(y[:], acc[m, s][:])
-                nc.sync.dma_start(out=out[m * M_TILE : (m + 1) * M_TILE, s * SLICE : (s + 1) * SLICE], in_=y[:])
+        for a in range(PASSES):
+            cast("s", w_bf[a], w_raw[a], 0, N)
+        for a in range(PASSES):
+            quant(w_words[a], w_bytes[a], w_bf[a], 0, N)
 
-        for a in range(PASSES - 1):
-            for j in range(PACK):
+        def evacuate(engine, queue, m, s):
+            y = keep.tile([M_TILE, SLICE], F32, name=f"y{m}{s}")
+            if engine == "s":
+                nc.scalar.copy(y[:], acc[m, s][:])
+            else:
+                nc.vector.tensor_copy(y[:], acc[m, s][:])
+            queue.dma_start(out=out[m * M_TILE : (m + 1) * M_TILE, s * SLICE : (s + 1) * SLICE], in_=y[:])
+
+        parts = ((0, 512), (512, 768))
+        last = PASSES - 1
+        def quant_part(a, part):
+            lo, hi = parts[part]
+            quant(g_words[a], g_bytes[a], gb[a], lo, hi)
+
+        for a in range(PASSES):
+            for j in range(PACK if a < last else PACK - 1):
                 gather(a, j, 0, S, T)
-            if a == 0:
-                for b in range(PASSES):
-                    cast("s", w_bf[b], w_raw[:, b, :, :], 0, N)
-                for b in range(PASSES):
-                    quant(w_words[b], w_bytes[b], w_bf[b], 0, N)
-            for lo, hi in ((0, 512), (512, 768)):
-                cast("s", gb[a], g4[a], lo, hi)
-                quant(g_words[a], g_bytes[a], gb[a], lo, hi)
-            for s in range(SLICES):
-                multiply(a, s)
-        a = PASSES - 1
-        for j in range(PACK - 1):
-            gather(a, j, 0, S, T)
+                if a > 0 and j == 0:
+                    quant_part(a - 1, 1)
+                    quant_part(a - 1, 0)
+                    for s in range(SLICES):
+                        multiply(a - 1, s)
+            if a < last:
+                cast("s", gb[a], g4[a], *parts[0])
+                cast("v", gb[a], g4[a], *parts[1])
         for s in range(SLICES):
             lo, hi = s * SLICE, (s + 1) * SLICE
-            gather(a, PACK - 1, lo, hi, T - S + hi)
-            cut = hi - SLICE // 2
-            cast("s", gb[a], g4[a], lo, cut)
-            cast("v", gb[a], g4[a], cut, hi)
-            quant(g_words[a], g_bytes[a], gb[a], lo, hi)
-            multiply(a, s)
-            finish(s)
+            gather(last, PACK - 1, lo, hi, T - S + hi)
+            if s < 2:
+                cast("s", gb[last], g4[last], lo, hi)
+        quant(g_words[last], g_bytes[last], gb[last], 0, SLICE)
+        multiply(last, 0)
+        cast("v", gb[last], g4[last], 2 * SLICE, S)
+        quant(g_words[last], g_bytes[last], gb[last], SLICE, 2 * SLICE)
+        multiply(last, 1)
+        quant(g_words[last], g_bytes[last], gb[last], 2 * SLICE, S)
+        multiply(last, 2)
+        for s in range(SLICES):
+            evacuate("s", nc.sync, 0, s)
+            evacuate("s" if s < 2 else "v", nc.scalar if s == 2 else nc.sync, 1, s)

from contextlib import ExitStack

import concourse.mybir as mybir

K, T, S, N = 1536, 2048, 768, 256
FLOPS = 2 * K * S * N

F32 = mybir.dt.float32
BF16 = mybir.dt.bfloat16
I32 = mybir.dt.int32
U32 = mybir.dt.uint32
U16 = mybir.dt.uint16
U8 = mybir.dt.uint8
FP8X4 = mybir.dt.float8_e4m3fn_x4
COPY = mybir.ActivationFunctionType.Copy

P = 128
PACK = 4
K_PASS = P * PACK
PASSES = K // K_PASS
M_TILE = 128
SLICE = 256
SLICES = S // SLICE


def tile_picked_pick_lin_none_srt_e_kernel(tc, xT, w, offs, out):
    nc = tc.nc
    with ExitStack() as ctx:
        keep = ctx.enter_context(tc.tile_pool(name="keep", bufs=1))
        psum = ctx.enter_context(tc.psum_pool(name="psum", bufs=1))

        offsets = keep.tile([P, S // 16], U16, name="offsets", align_bytes=64)
        x_raw = [[keep.tile([P, T], F32, name=f"x_raw{a}{j}", align_bytes=64) for j in range(PACK)] for a in range(PASSES)]
        g4 = [keep.tile([P, PACK, S], F32, name=f"g4_{a}", align_bytes=64) for a in range(PASSES)]
        gb = [keep.tile([P, S, PACK], BF16, name=f"gb{a}", align_bytes=64) for a in range(PASSES)]
        g_words = [keep.tile([P, S], U32, name=f"g_words{a}", align_bytes=64) for a in range(PASSES)]
        g_bytes = [keep.tile([P, S], U8, name=f"g_bytes{a}", align_bytes=64) for a in range(PASSES)]
        w_raw = [keep.tile([P, PACK, N], F32, name=f"w_raw{a}", align_bytes=64) for a in range(PASSES)]
        w_bf = [keep.tile([P, N, PACK], BF16, name=f"w_bf{a}", align_bytes=64) for a in range(PASSES)]
        w_words = [keep.tile([P, N], U32, name=f"w_words{a}", align_bytes=64) for a in range(PASSES)]
        w_bytes = [keep.tile([P, N], U8, name=f"w_bytes{a}", align_bytes=64) for a in range(PASSES)]

        def load_w(a):
            nc.sync.dma_start(out=w_raw[a][:], in_=w[a * K_PASS : (a + 1) * K_PASS, :].rearrange("(p j) m -> p j m", j=PACK))

        def load_x(a, j, lo, hi):
            rows = xT[a * K_PASS : (a + 1) * K_PASS, lo:hi].rearrange("(p j) c -> p j c", j=PACK)
            nc.sync.dma_start(out=x_raw[a][j][:, lo:hi], in_=rows[:, j, :])

        for a in range(PASSES):
            load_w(a)
        nc.sync.dma_start(offsets[:], offs)
        for a in range(PASSES):
            for j in range(PACK):
                cuts = (0, T - 2 * SLICE, T - SLICE, T) if (a, j) == (PASSES - 1, PACK - 1) else (0, T)
                for lo, hi in zip(cuts[:-1], cuts[1:]):
                    load_x(a, j, lo, hi)

        def cast(engine, dst, src, lo, hi, j0=0, j1=PACK):
            o = dst[:, lo:hi, j0:j1].rearrange("p (c i) t -> p c t i", i=4)
            i = src[:, j0:j1, lo:hi].rearrange("p t (c i) -> p c t i", i=4)
            if engine == "s":
                nc.scalar.activation(o, i, COPY)
            else:
                nc.vector.tensor_copy(o, i)

        def quant(words, scales, bf, lo, hi):
            nc.vector.quantize_mx(
                out=words[:, lo:hi].bitcast(FP8X4),
                scales=scales[:, lo:hi],
                in_=bf[:, lo:hi, :].rearrange("p c t -> p (c t)"),
            )

        def gather(a, j, lo, hi, window):
            picks = offsets[:, lo // 16 : hi // 16]
            nc.vector.tensor_copy(g4[a][:, j, lo:hi], x_raw[a][j][:, 0:window].indirect(picks))

        acc = {}
        for s in range(SLICES):
            for m in range(N // M_TILE):
                acc[m, s] = psum.tile([M_TILE, SLICE], F32, name=f"acc{m}{s}")

        def multiply(a, s):
            for m in range(N // M_TILE):
                mc = slice(m * M_TILE, (m + 1) * M_TILE)
                jc = slice(s * SLICE, (s + 1) * SLICE)
                nc.tensor.matmul_mx(
                    out=acc[m, s][:],
                    lhsT=w_words[a][:, mc].bitcast(FP8X4),
                    lhsT_scale=w_bytes[a][:, mc],
                    rhs=g_words[a][:, jc].bitcast(FP8X4),
                    rhs_scale=g_bytes[a][:, jc],
                    start=(a == 0),
                    stop=(a == PASSES - 1),
                )

        for a in range(PASSES):
            cast("s", w_bf[a], w_raw[a], 0, N)
        for a in range(PASSES):
            quant(w_words[a], w_bytes[a], w_bf[a], 0, N)

        def evacuate(engine, queue, m, s):
            y = keep.tile([M_TILE, SLICE], F32, name=f"y{m}{s}")
            if engine == "s":
                nc.scalar.copy(y[:], acc[m, s][:])
            else:
                nc.vector.tensor_copy(y[:], acc[m, s][:])
            queue.dma_start(out=out[m * M_TILE : (m + 1) * M_TILE, s * SLICE : (s + 1) * SLICE], in_=y[:])

        parts = ((0, 512), (512, 768))
        last = PASSES - 1
        def quant_part(a, part):
            lo, hi = parts[part]
            quant(g_words[a], g_bytes[a], gb[a], lo, hi)

        for a in range(PASSES):
            for j in range(PACK if a < last else PACK - 1):
                gather(a, j, 0, S, T)
                if a > 0 and j == 0:
                    quant_part(a - 1, 1)
                    quant_part(a - 1, 0)
                    for s in range(SLICES):
                        multiply(a - 1, s)
            if a < last:
                cast("s", gb[a], g4[a], *parts[0])
                cast("v", gb[a], g4[a], *parts[1])
        for s in range(SLICES):
            lo, hi = s * SLICE, (s + 1) * SLICE
            gather(last, PACK - 1, lo, hi, T - S + hi)
            if s < 2:
                cast("s", gb[last], g4[last], lo, hi)
        quant(g_words[last], g_bytes[last], gb[last], 0, SLICE)
        multiply(last, 0)
        cast("v", gb[last], g4[last], 2 * SLICE, S)
        quant(g_words[last], g_bytes[last], gb[last], SLICE, 2 * SLICE)
        multiply(last, 1)
        quant(g_words[last], g_bytes[last], gb[last], 2 * SLICE, S)
        multiply(last, 2)
        for s in range(SLICES):
            evacuate("s", nc.sync, 0, s)
            evacuate("s" if s < 2 else "v", nc.scalar if s == 2 else nc.sync, 1, s)
